import numpy as np
import ml_dtypes


def mxq(x, axis, fmt="e4m3"):
    dtype, down = {"e4m3": (ml_dtypes.float8_e4m3fn, 7), "e5m2": (ml_dtypes.float8_e5m2, 14)}[fmt]
    v = np.moveaxis(np.asarray(x, np.float32).astype(ml_dtypes.bfloat16).astype(np.float64), axis, -1)
    blocks = v.reshape(v.shape[:-1] + (-1, 32))
    amax = np.abs(blocks).max(-1, keepdims=True)
    byte = np.maximum(np.where(amax > 0, np.frexp(amax)[1] - 1 + 127, 0) - down, 1)
    scale = np.exp2(byte - 127.0)
    codes = (blocks / scale).astype(np.float32).astype(dtype).astype(np.float64)
    return np.moveaxis((codes * scale).reshape(v.shape), -1, axis)


WIDE = False


def mx_kscale(k):
    if not WIDE:
        return np.ones(k)
    levels = np.array([10, -10, 5, -5, 0])
    if k % 512:
        return np.exp2(np.random.permutation(np.resize(levels, k // 32))).repeat(32)
    a = np.empty((k // 512, 16))
    for p in range(k // 512):
        a[p, :8] = np.random.permutation(np.resize(levels, 8))
        for g in range(8):
            far = levels[np.abs(levels - a[p, g]) >= 10]
            a[p, g + 8] = far[np.random.randint(len(far))]
    return np.exp2(a.ravel()).repeat(32)


def f64(x):
    return np.asarray(x).astype(np.float64)


def striped(idx):
    return np.tile(idx.reshape(-1, 16).T, (8, 1)).astype(np.uint16)


def unstriped(offs):
    return offs[:16].T.reshape(-1).astype(np.int64)


E2M1 = np.array([0.0, 0.5, 1.0, 1.5, 2.0, 3.0, 4.0, 6.0, -0.0, -0.5, -1.0, -1.5, -2.0, -3.0, -4.0, -6.0])


def pack_weight(w, fmt):
    k, n = w.shape
    w = f64(np.asarray(w, np.float32).astype(ml_dtypes.bfloat16)).reshape(k // 32, 32, n)
    amax = np.abs(w).max(1)
    if fmt == "e4m3":
        byte = np.frexp(amax)[1] - 1 + 127 - 7
    else:
        mant, ex = np.frexp(amax / 6.0)
        byte = np.where(mant > 0.5, ex, ex - 1) + 127
    byte = np.clip(np.where(amax > 0, byte, 1), 1, 254)
    scaled = (w * np.exp2(127.0 - byte)[:, None, :]).reshape(k, n).astype(np.float32)
    by_word = np.ascontiguousarray(scaled.reshape(k // 512, 128, 4, n).transpose(0, 1, 3, 2))
    if fmt == "e4m3":
        words = by_word.astype(ml_dtypes.float8_e4m3fn).view(np.uint8)
    else:
        c = by_word.astype(ml_dtypes.float4_e2m1fn).view(np.uint8) & 0xF
        words = (c[..., 0::2] | (c[..., 1::2] << 4)).reshape(k // 512, 128, 2 * n)
    return np.ascontiguousarray(words), np.ascontiguousarray(byte.astype(np.uint8).reshape(k // 512, 16, n))


def unpack_weight(words, scales, fmt):
    g, _, n = scales.shape
    words = np.ascontiguousarray(words).reshape(g, 128, n, -1)
    if fmt == "e4m3":
        vals = words.view(ml_dtypes.float8_e4m3fn).astype(np.float64)
    else:
        nib = np.empty((g, 128, n, 4), np.uint8)
        nib[..., 0::2] = words & 0xF
        nib[..., 1::2] = words >> 4
        vals = E2M1[nib]
    vals = vals * np.repeat(np.exp2(scales.astype(np.float64) - 127.0), 8, axis=1)[..., None]
    return vals.transpose(0, 1, 3, 2).reshape(g * 512, n)


def pack_table4(v):
    words, scales = pack_weight(v, "e2m1")
    g, t = words.shape[0] // 2, v.shape[1]
    words = words.reshape(g, 2, 128, t, 2).transpose(0, 2, 3, 1, 4)
    return np.concatenate([words.reshape(g, -1), scales.reshape(g, -1)], axis=1)


def unpack_table4(tab):
    g, t = tab.shape[0], tab.shape[1] // 544
    words = tab[:, :512 * t].reshape(g, 128, t, 2, 2).transpose(0, 3, 1, 2, 4).reshape(2 * g, 128, 2 * t)
    return unpack_weight(words, tab[:, 512 * t:].reshape(2 * g, 16, t), "e2m1")


K, M, T, S = 3072, 512, 1024, 512


def setup_inputs():
    n = np.random.standard_normal
    s = mx_kscale(K)[:, None]
    return {
        "tab": pack_table4(n((K, T)) * s),
        "w": (n((K, M)) / np.sqrt(K) / s).astype(np.float32),
        "offs": striped(np.random.permutation(T)[:S]),
    }


def reference(tab, w, offs):
    tab_ = unpack_table4(tab)[:, unstriped(offs)]
    w_ = mxq(f64(w), 0, "e4m3")
    y = w_.T @ tab_
    return y

@@ -1,0 +1,156 @@
+from contextlib import ExitStack
+
+import concourse.mybir as mybir
+
+F32 = mybir.dt.float32
+BF16 = mybir.dt.bfloat16
+I32 = mybir.dt.int32
+U32 = mybir.dt.uint32
+U16 = mybir.dt.uint16
+U8 = mybir.dt.uint8
+FP8X4 = mybir.dt.float8_e4m3fn_x4
+FP4X4 = mybir.dt.float4_e2m1fn_x4
+
+K, M, T, S = 3072, 512, 1024, 512
+P = 128
+K_PASS = 512
+PASSES = K // K_PASS
+PAIRS = PASSES // 2
+FLOPS = 2 * K * M * S
+
+
+def tile_list_tab4_none_kernel(tc, tab, w, offs, out):
+    nc = tc.nc
+    with ExitStack() as ctx:
+        keep = ctx.enter_context(tc.tile_pool(name="keep", bufs=1))
+        psum = ctx.enter_context(tc.psum_pool(name="psum", bufs=1))
+
+        offsets = keep.tile([P, S // 16], U16, name="offsets")
+        nc.sync.dma_start(offsets[:], offs)
+
+        scale_table = [keep.tile([P, T], U8, name=f"scale_table{h}", align_bytes=64) for h in range(2)]
+        nc.vector.memset(scale_table[0][:].bitcast(I32), 0)
+        nc.gpsimd.memset(scale_table[1][:].bitcast(I32), 0)
+        shifted = [keep.tile([P, 2, S], U8, name=f"shifted{m}", align_bytes=64) for m in range(1, PAIRS)]
+
+        def load_words(m):
+            t = keep.tile([P, T], I32, name=f"words{m}", align_bytes=64)
+            nc.sync.dma_start(t[:], tab[m, 0 : 512 * T].bitcast(I32).rearrange("(p t) -> p t", p=P))
+            return t
+
+        def load_w(a, c0, c1):
+            t = keep.tile([P, 4, c1 - c0], F32, name=f"raw{a}_{c0}", align_bytes=64)
+            nc.sync.dma_start(t[:], w[K_PASS * a : K_PASS * (a + 1), c0:c1].rearrange("(p j) c -> p j c", j=4))
+            return t
+
+        def load_scales(h, q):
+            row = 16 * h + 4 * q
+            src = tab[:, 512 * T + row * T : 512 * T + (row + 4) * T].bitcast(I32)
+            queue = nc.gpsimd if h else nc.scalar
+            queue.dma_start(
+                scale_table[h][32 * q : 32 * q + 4 * PAIRS, :].bitcast(I32),
+                src.rearrange("m (r t) -> m r t", r=4),
+            )
+
+        words = [None] * PAIRS
+        raw = [None] * PASSES
+        for h in range(2):
+            for q in range(4):
+                load_scales(h, q)
+        for t in shifted:
+            nc.gpsimd.memset(t[:].bitcast(I32), 0)
+        raw[0] = [load_w(0, 0, M // 2)]
+        words[0] = load_words(0)
+        raw[0] += [load_w(0, M // 2, M)]
+        raw[1] = [load_w(1, 0, M)]
+        words[1] = load_words(1)
+        raw[2] = [load_w(2, 0, M)]
+        words[2] = load_words(2)
+        raw[3] = [load_w(3, 0, M)]
+        raw[4] = [load_w(4, 0, M)]
+        raw[5] = [load_w(5, 0, M // 2), load_w(5, M // 2, M)]
+
+        picked_scales = keep.tile([P, 2, S], U8, name="picked_scales", align_bytes=64)
+
+        def pick_scales(h):
+            nc.vector.tensor_copy(picked_scales[:, h, :], scale_table[h][:].indirect(offsets[:]))
+
+        def shift_scales(m):
+            nc.sync.dma_start(
+                shifted[m - 1][0:112, :, :].bitcast(I32), picked_scales[4 * m : 4 * m + 112, :, :].bitcast(I32)
+            )
+
+        parted = []
+
+        def pick_words(m):
+            g = keep.tile([P, S], I32, name=f"picked{m}", align_bytes=64)
+            nc.vector.tensor_copy(g[:].bitcast(U32), words[m][:].bitcast(U32).indirect(offsets[:]))
+            d = keep.tile([P, 2, 2 * S], U8, name=f"parted{m}", align_bytes=64)
+            nc.vector.tensor_copy(d[:].bitcast(U16), g[:].bitcast(U16).rearrange("p (j h) -> p h j", h=2))
+            parted.append(d)
+
+        def interleave(copy, dst, src, d0, s0, n):
+            copy(
+                out=dst[:, d0 : d0 + n, :].rearrange("p (c i) t -> p c t i", i=4),
+                in_=src[:, :, s0 : s0 + n].rearrange("p t (c i) -> p c t i", i=4),
+            )
+
+        banks = [psum.tile([P, S], F32, name=f"bank{n}") for n in range(4)]
+
+        def quantise(a, grouped, c0, c1):
+            codes = keep.tile([P, c1 - c0], U32, name=f"codes{a}_{c0}", align_bytes=64)
+            scales = keep.tile([P, c1 - c0], U8, name=f"scales{a}_{c0}", align_bytes=64)
+            nc.vector.quantize_mx(out=codes[:].bitcast(FP8X4), scales=scales[:], in_=grouped[:].rearrange("p c t -> p (c t)"))
+            return codes, scales
+
+        def multiply(a, n, codes, scales, c):
+            m, h = a // 2, a % 2
+            moving_scales = shifted[m - 1] if m else picked_scales
+            nc.tensor.matmul_mx(
+                out=banks[n][:],
+                lhsT=codes[:, c : c + P].bitcast(FP8X4),
+                lhsT_scale=scales[:, c : c + P],
+                rhs=parted[m][:, h, :].bitcast(FP4X4),
+                rhs_scale=moving_scales[:, h, :],
+                start=(a == 0),
+                stop=(a == PASSES - 1),
+            )
+
+        pick_scales(0)
+        pick_words(0)
+        pick_scales(1)
+        shift_scales(1)
+        shift_scales(2)
+        for a in range(PASSES - 1):
+            if a in (1, 2):
+                pick_words(a)
+            grouped = keep.tile([P, M, 4], BF16, name=f"grouped{a}", align_bytes=64)
+            if a == 0:
+                for i in range(2):
+                    interleave(nc.scalar.copy, grouped, raw[a][i], M // 2 * i, 0, M // 2)
+            else:
+                split = 512 if a < 4 else 256
+                interleave(nc.scalar.copy, grouped, raw[a][0], 0, 0, split)
+                if split < M:
+                    interleave(nc.vector.tensor_copy, grouped, raw[a][0], split, split, M - split)
+            codes, scales = quantise(a, grouped, 0, M)
+            for n in range(4):
+                multiply(a, n, codes, scales, P * n)
+
+        a = PASSES - 1
+        for half in range(2):
+            pieces = []
+            for i, copy in ((0, nc.scalar.copy), (1, nc.vector.tensor_copy)):
+                grouped = keep.tile([P, P, 4], BF16, name=f"last{half}_{i}", align_bytes=64)
+                interleave(copy, grouped, raw[a][half], 0, P * i, P)
+                pieces.append(grouped)
+            for i in (1, 0):
+                n = 2 * half + i
+                codes, scales = quantise(a, pieces[i], P * n, P * n + P)
+                multiply(a, n, codes, scales, 0)
+                result = keep.tile([P, S], F32, name=f"result{n}")
+                if i:
+                    nc.vector.tensor_copy(result[:], banks[n][:])
+                else:
+                    nc.scalar.copy(result[:], banks[n][:])
+                nc.sync.dma_start(out[P * n : P * n + P, :], result[:])

@@ -26,12 +26,15 @@ def tile_list_tab4_none_kernel(tc, tab, w, offs, out):
         psum = ctx.enter_context(tc.psum_pool(name="psum", bufs=1))
 
         offsets = keep.tile([P, S // 16], U16, name="offsets")
-        nc.sync.dma_start(offsets[:], offs)
 
-        scale_table = [keep.tile([P, T], U8, name=f"scale_table{h}", align_bytes=64) for h in range(2)]
-        nc.vector.memset(scale_table[0][:].bitcast(I32), 0)
-        nc.gpsimd.memset(scale_table[1][:].bitcast(I32), 0)
-        shifted = [keep.tile([P, 2, S], U8, name=f"shifted{m}", align_bytes=64) for m in range(1, PAIRS)]
+        nc.sync.dma_start(offsets[:], offs)
+        scale_table = keep.tile([P, PAIRS, T], U8, name="scale_table", align_bytes=64)
+        shifted = keep.tile([P, PAIRS, S], U8, name="shifted", align_bytes=64)
+        nc.gpsimd.memset(scale_table[:].bitcast(I32), 0)
+        nc.vector.memset(shifted[:].bitcast(I32), 0)
+        warm = keep.tile([P, 2], F32, name="warm")
+        nc.vector.memset(warm[:, 0:1], 0.0)
+        nc.scalar.copy(warm[:, 1:2], warm[:, 0:1])
 
         def load_words(m):
             t = keep.tile([P, T], I32, name=f"words{m}", align_bytes=64)
@@ -43,51 +46,46 @@ def tile_list_tab4_none_kernel(tc, tab, w, offs, out):
             nc.sync.dma_start(t[:], w[K_PASS * a : K_PASS * (a + 1), c0:c1].rearrange("(p j) c -> p j c", j=4))
             return t
 
-        def load_scales(h, q):
-            row = 16 * h + 4 * q
-            src = tab[:, 512 * T + row * T : 512 * T + (row + 4) * T].bitcast(I32)
-            queue = nc.gpsimd if h else nc.scalar
-            queue.dma_start(
-                scale_table[h][32 * q : 32 * q + 4 * PAIRS, :].bitcast(I32),
-                src.rearrange("m (r t) -> m r t", r=4),
-            )
+        def load_scales(q):
+            first = 512 * T + 4 * q * T
+            src = tab[:, first : first + 20 * T].bitcast(I32).rearrange("m (i t) -> i m t", i=20)
+            nc.scalar.dma_start(scale_table[32 * q : 32 * q + 20, :, :].bitcast(I32), src)
 
         words = [None] * PAIRS
         raw = [None] * PASSES
-        for h in range(2):
-            for q in range(4):
-                load_scales(h, q)
-        for t in shifted:
-            nc.gpsimd.memset(t[:].bitcast(I32), 0)
-        raw[0] = [load_w(0, 0, M // 2)]
         words[0] = load_words(0)
-        raw[0] += [load_w(0, M // 2, M)]
-        raw[1] = [load_w(1, 0, M)]
+        raw[0] = [load_w(0, 0, M // 2), load_w(0, M // 2, M)]
+        for q in range(4):
+            load_scales(q)
         words[1] = load_words(1)
+        raw[1] = [load_w(1, 0, M)]
         raw[2] = [load_w(2, 0, M)]
         words[2] = load_words(2)
         raw[3] = [load_w(3, 0, M)]
         raw[4] = [load_w(4, 0, M)]
         raw[5] = [load_w(5, 0, M // 2), load_w(5, M // 2, M)]
 
-        picked_scales = keep.tile([P, 2, S], U8, name="picked_scales", align_bytes=64)
+        picked_scales = keep.tile([P, PAIRS, S], U8, name="picked_scales", align_bytes=64)
 
-        def pick_scales(h):
-            nc.vector.tensor_copy(picked_scales[:, h, :], scale_table[h][:].indirect(offsets[:]))
+        def pick_scales(m):
+            nc.vector.tensor_copy(picked_scales[:, m, :], scale_table[:, m, :].indirect(offsets[:]))
 
-        def shift_scales(m):
-            nc.sync.dma_start(
-                shifted[m - 1][0:112, :, :].bitcast(I32), picked_scales[4 * m : 4 * m + 112, :, :].bitcast(I32)
-            )
-
+        picked = []
         parted = []
 
         def pick_words(m):
             g = keep.tile([P, S], I32, name=f"picked{m}", align_bytes=64)
             nc.vector.tensor_copy(g[:].bitcast(U32), words[m][:].bitcast(U32).indirect(offsets[:]))
+            picked.append(g)
+
+        def part_words(m):
             d = keep.tile([P, 2, 2 * S], U8, name=f"parted{m}", align_bytes=64)
-            nc.vector.tensor_copy(d[:].bitcast(U16), g[:].bitcast(U16).rearrange("p (j h) -> p h j", h=2))
+            nc.vector.tensor_copy(d[:].bitcast(U16), picked[m][:].bitcast(U16).rearrange("p (j h) -> p h j", h=2))
             parted.append(d)
+
+        def pick(m):
+            pick_words(m)
+            part_words(m)
 
         def interleave(copy, dst, src, d0, s0, n):
             copy(
@@ -105,31 +103,31 @@ def tile_list_tab4_none_kernel(tc, tab, w, offs, out):
 
         def multiply(a, n, codes, scales, c):
             m, h = a // 2, a % 2
-            moving_scales = shifted[m - 1] if m else picked_scales
+            moving_scales = shifted if h else picked_scales
             nc.tensor.matmul_mx(
                 out=banks[n][:],
                 lhsT=codes[:, c : c + P].bitcast(FP8X4),
                 lhsT_scale=scales[:, c : c + P],
                 rhs=parted[m][:, h, :].bitcast(FP4X4),
-                rhs_scale=moving_scales[:, h, :],
+                rhs_scale=moving_scales[:, m, :],
                 start=(a == 0),
                 stop=(a == PASSES - 1),
             )
 
-        pick_scales(0)
         pick_words(0)
-        pick_scales(1)
-        shift_scales(1)
-        shift_scales(2)
+        for m in range(PAIRS):
+            pick_scales(m)
+        nc.sync.dma_start(shifted[0:112, :, :].bitcast(I32), picked_scales[16:128, :, :].bitcast(I32))
+        part_words(0)
         for a in range(PASSES - 1):
             if a in (1, 2):
-                pick_words(a)
+                pick(a)
             grouped = keep.tile([P, M, 4], BF16, name=f"grouped{a}", align_bytes=64)
             if a == 0:
                 for i in range(2):
                     interleave(nc.scalar.copy, grouped, raw[a][i], M // 2 * i, 0, M // 2)
             else:
-                split = 512 if a < 4 else 256
+                split = (512, 512, 512, 448, 384)[a]
                 interleave(nc.scalar.copy, grouped, raw[a][0], 0, 0, split)
                 if split < M:
                     interleave(nc.vector.tensor_copy, grouped, raw[a][0], split, split, M - split)

@@ -26,129 +26,131 @@ def tile_list_tab4_none_kernel(tc, tab, w, offs, out):
         psum = ctx.enter_context(tc.psum_pool(name="psum", bufs=1))
 
         offsets = keep.tile([P, S // 16], U16, name="offsets")
-
         nc.sync.dma_start(offsets[:], offs)
+
         scale_table = keep.tile([P, PAIRS, T], U8, name="scale_table", align_bytes=64)
-        shifted = keep.tile([P, PAIRS, S], U8, name="shifted", align_bytes=64)
         nc.gpsimd.memset(scale_table[:].bitcast(I32), 0)
-        nc.vector.memset(shifted[:].bitcast(I32), 0)
+        shifted = keep.tile([P, PAIRS, S], U8, name="shifted", align_bytes=64)
+        nc.gpsimd.memset(shifted[:].bitcast(I32), 0)
+        picked_scales = keep.tile([P, PAIRS, S], U8, name="picked_scales", align_bytes=64)
         warm = keep.tile([P, 2], F32, name="warm")
         nc.vector.memset(warm[:, 0:1], 0.0)
         nc.scalar.copy(warm[:, 1:2], warm[:, 0:1])
 
-        def load_words(m):
-            t = keep.tile([P, T], I32, name=f"words{m}", align_bytes=64)
-            nc.sync.dma_start(t[:], tab[m, 0 : 512 * T].bitcast(I32).rearrange("(p t) -> p t", p=P))
-            return t
+        banks = [psum.tile([P, S], F32, name=f"bank{n}") for n in range(4)]
+        words, parted, raw, grouped, codes, scales = {}, {}, {}, {}, {}, {}
 
-        def load_w(a, c0, c1):
-            t = keep.tile([P, 4, c1 - c0], F32, name=f"raw{a}_{c0}", align_bytes=64)
-            nc.sync.dma_start(t[:], w[K_PASS * a : K_PASS * (a + 1), c0:c1].rearrange("(p j) c -> p j c", j=4))
-            return t
+        def load_words(m):
+            words[m] = keep.tile([P, T], I32, name=f"words{m}", align_bytes=64)
+            nc.sync.dma_start(words[m][:], tab[m, 0 : 512 * T].bitcast(I32).rearrange("(p t) -> p t", p=P))
 
         def load_scales(q):
             first = 512 * T + 4 * q * T
             src = tab[:, first : first + 20 * T].bitcast(I32).rearrange("m (i t) -> i m t", i=20)
-            nc.scalar.dma_start(scale_table[32 * q : 32 * q + 20, :, :].bitcast(I32), src)
+            nc.sync.dma_start(scale_table[32 * q : 32 * q + 20, :, :].bitcast(I32), src)
 
-        words = [None] * PAIRS
-        raw = [None] * PASSES
-        words[0] = load_words(0)
-        raw[0] = [load_w(0, 0, M // 2), load_w(0, M // 2, M)]
-        for q in range(4):
-            load_scales(q)
-        words[1] = load_words(1)
-        raw[1] = [load_w(1, 0, M)]
-        raw[2] = [load_w(2, 0, M)]
-        words[2] = load_words(2)
-        raw[3] = [load_w(3, 0, M)]
-        raw[4] = [load_w(4, 0, M)]
-        raw[5] = [load_w(5, 0, M // 2), load_w(5, M // 2, M)]
+        def load_weights(a, c0, c1):
+            key = (a, c0)
+            raw[key] = keep.tile([P, 4, c1 - c0], F32, name=f"raw{a}_{c0}", align_bytes=64)
+            rows = w[K_PASS * a : K_PASS * (a + 1), c0:c1]
+            nc.sync.dma_start(raw[key][:], rows.rearrange("(p j) c -> p j c", j=4))
 
-        picked_scales = keep.tile([P, PAIRS, S], U8, name="picked_scales", align_bytes=64)
+        def pick_words(m):
+            picked = keep.tile([P, S], I32, name=f"picked{m}", align_bytes=64)
+            nc.vector.tensor_copy(picked[:].bitcast(U32), words[m][:].bitcast(U32).indirect(offsets[:]))
+            parted[m] = keep.tile([P, 2, 2 * S], U8, name=f"parted{m}", align_bytes=64)
+            nc.vector.tensor_copy(parted[m][:].bitcast(U16), picked[:].bitcast(U16).rearrange("p (j h) -> p h j", h=2))
 
         def pick_scales(m):
             nc.vector.tensor_copy(picked_scales[:, m, :], scale_table[:, m, :].indirect(offsets[:]))
 
-        picked = []
-        parted = []
+        def shift_scales(m0, m1):
+            nc.sync.dma_start(shifted[0:112, m0:m1, :].bitcast(I32), picked_scales[16:128, m0:m1, :].bitcast(I32))
 
-        def pick_words(m):
-            g = keep.tile([P, S], I32, name=f"picked{m}", align_bytes=64)
-            nc.vector.tensor_copy(g[:].bitcast(U32), words[m][:].bitcast(U32).indirect(offsets[:]))
-            picked.append(g)
+        def interleave(copy, a, r0, g0, c0, c1):
+            if (a, g0) not in grouped:
+                width = M if g0 == 0 and (a, M // 2) not in raw or a == 0 else M // 2
+                grouped[a, g0] = keep.tile([P, width, 4], BF16, name=f"grouped{a}_{g0}", align_bytes=64)
+            dst = grouped[a, g0][:, c0 - g0 : c1 - g0, :].rearrange("p (c i) t -> p c t i", i=4)
+            src = raw[a, r0][:, :, c0 - r0 : c1 - r0].rearrange("p t (c i) -> p c t i", i=4)
+            copy(out=dst, in_=src)
 
-        def part_words(m):
-            d = keep.tile([P, 2, 2 * S], U8, name=f"parted{m}", align_bytes=64)
-            nc.vector.tensor_copy(d[:].bitcast(U16), picked[m][:].bitcast(U16).rearrange("p (j h) -> p h j", h=2))
-            parted.append(d)
+        def quantise(a, g0, c0, c1):
+            key = (a, c0)
+            codes[key] = keep.tile([P, c1 - c0], U32, name=f"codes{a}_{c0}", align_bytes=64)
+            scales[key] = keep.tile([P, c1 - c0], U8, name=f"scales{a}_{c0}", align_bytes=64)
+            in_ = grouped[a, g0][:, c0 - g0 : c1 - g0, :].rearrange("p c t -> p (c t)")
+            nc.vector.quantize_mx(out=codes[key][:].bitcast(FP8X4), scales=scales[key][:], in_=in_)
 
-        def pick(m):
-            pick_words(m)
-            part_words(m)
-
-        def interleave(copy, dst, src, d0, s0, n):
-            copy(
-                out=dst[:, d0 : d0 + n, :].rearrange("p (c i) t -> p c t i", i=4),
-                in_=src[:, :, s0 : s0 + n].rearrange("p t (c i) -> p c t i", i=4),
-            )
-
-        banks = [psum.tile([P, S], F32, name=f"bank{n}") for n in range(4)]
-
-        def quantise(a, grouped, c0, c1):
-            codes = keep.tile([P, c1 - c0], U32, name=f"codes{a}_{c0}", align_bytes=64)
-            scales = keep.tile([P, c1 - c0], U8, name=f"scales{a}_{c0}", align_bytes=64)
-            nc.vector.quantize_mx(out=codes[:].bitcast(FP8X4), scales=scales[:], in_=grouped[:].rearrange("p c t -> p (c t)"))
-            return codes, scales
-
-        def multiply(a, n, codes, scales, c):
+        def multiply(a, c0, c1):
             m, h = a // 2, a % 2
             moving_scales = shifted if h else picked_scales
-            nc.tensor.matmul_mx(
-                out=banks[n][:],
-                lhsT=codes[:, c : c + P].bitcast(FP8X4),
-                lhsT_scale=scales[:, c : c + P],
-                rhs=parted[m][:, h, :].bitcast(FP4X4),
-                rhs_scale=moving_scales[:, m, :],
-                start=(a == 0),
-                stop=(a == PASSES - 1),
-            )
+            for c in range(0, c1 - c0, P):
+                nc.tensor.matmul_mx(
+                    out=banks[(c0 + c) // P][:],
+                    lhsT=codes[a, c0][:, c : c + P].bitcast(FP8X4),
+                    lhsT_scale=scales[a, c0][:, c : c + P],
+                    rhs=parted[m][:, h, :].bitcast(FP4X4),
+                    rhs_scale=moving_scales[:, m, :],
+                    start=(a == 0),
+                    stop=(a == PASSES - 1),
+                )
+
+        def store(copy, n):
+            result = keep.tile([P, S], F32, name=f"result{n}")
+            copy(result[:], banks[n][:])
+            nc.sync.dma_start(out[P * n : P * n + P, :], result[:])
+
+        on_scalar, on_vector = nc.scalar.copy, nc.vector.tensor_copy
+        H = M // 2
+
+        load_words(0)
+        load_weights(0, 0, H)
+        load_weights(0, H, M)
+        for q in range(4):
+            load_scales(q)
+        load_words(1)
+        load_weights(1, 0, M)
+        load_weights(2, 0, M)
 
         pick_words(0)
-        for m in range(PAIRS):
-            pick_scales(m)
-        nc.sync.dma_start(shifted[0:112, :, :].bitcast(I32), picked_scales[16:128, :, :].bitcast(I32))
-        part_words(0)
-        for a in range(PASSES - 1):
-            if a in (1, 2):
-                pick(a)
-            grouped = keep.tile([P, M, 4], BF16, name=f"grouped{a}", align_bytes=64)
-            if a == 0:
-                for i in range(2):
-                    interleave(nc.scalar.copy, grouped, raw[a][i], M // 2 * i, 0, M // 2)
-            else:
-                split = (512, 512, 512, 448, 384)[a]
-                interleave(nc.scalar.copy, grouped, raw[a][0], 0, 0, split)
-                if split < M:
-                    interleave(nc.vector.tensor_copy, grouped, raw[a][0], split, split, M - split)
-            codes, scales = quantise(a, grouped, 0, M)
-            for n in range(4):
-                multiply(a, n, codes, scales, P * n)
+        pick_scales(0)
+        shift_scales(0, 1)
+        interleave(on_scalar, 0, 0, 0, 0, H)
+        interleave(on_scalar, 0, H, 0, H, M)
+        quantise(0, 0, 0, M)
+        multiply(0, 0, M)
 
-        a = PASSES - 1
-        for half in range(2):
-            pieces = []
-            for i, copy in ((0, nc.scalar.copy), (1, nc.vector.tensor_copy)):
-                grouped = keep.tile([P, P, 4], BF16, name=f"last{half}_{i}", align_bytes=64)
-                interleave(copy, grouped, raw[a][half], 0, P * i, P)
-                pieces.append(grouped)
-            for i in (1, 0):
-                n = 2 * half + i
-                codes, scales = quantise(a, pieces[i], P * n, P * n + P)
-                multiply(a, n, codes, scales, 0)
-                result = keep.tile([P, S], F32, name=f"result{n}")
-                if i:
-                    nc.vector.tensor_copy(result[:], banks[n][:])
-                else:
-                    nc.scalar.copy(result[:], banks[n][:])
-                nc.sync.dma_start(out[P * n : P * n + P, :], result[:])
+        load_words(2)
+        load_weights(3, 0, M)
+        pick_scales(1)
+        pick_scales(2)
+        shift_scales(1, 3)
+        for c0 in (0, H):
+            load_weights(4, c0, c0 + H)
+            load_weights(5, c0, c0 + H)
+
+        pick_words(1)
+        for a in (1, 2):
+            interleave(on_scalar, a, 0, 0, 0, M)
+            quantise(a, 0, 0, M)
+            multiply(a, 0, M)
+        pick_words(2)
+
+        interleave(on_scalar, 3, 0, 0, 0, H)
+        interleave(on_scalar, 3, 0, 0, H, 448)
+        interleave(on_vector, 3, 0, 0, 448, M)
+        for c0 in (0, H):
+            quantise(3, 0, c0, c0 + H)
+            multiply(3, c0, c0 + H)
+
+        for c0 in (0, H):
+            for a in (4, 5):
+                split = c0 + (160 if c0 and a == 5 else 192)
+                interleave(on_scalar, a, c0, c0, c0, split)
+                interleave(on_vector, a, c0, c0, split, c0 + H)
+                quantise(a, c0, c0, c0 + H)
+                multiply(a, c0, c0 + H)
+        for n in range(3):
+            store(on_scalar, n)
+        store(on_vector, 3)

@@ -16,6 +16,7 @@ P = 128
 K_PASS = 512
 PASSES = K // K_PASS
 PAIRS = PASSES // 2
+H = M // 2
 FLOPS = 2 * K * M * S
 
 
@@ -69,7 +70,7 @@ def tile_list_tab4_none_kernel(tc, tab, w, offs, out):
 
         def interleave(copy, a, r0, g0, c0, c1):
             if (a, g0) not in grouped:
-                width = M if g0 == 0 and (a, M // 2) not in raw or a == 0 else M // 2
+                width = M if a < 3 else P if a == 5 and g0 else H
                 grouped[a, g0] = keep.tile([P, width, 4], BF16, name=f"grouped{a}_{g0}", align_bytes=64)
             dst = grouped[a, g0][:, c0 - g0 : c1 - g0, :].rearrange("p (c i) t -> p c t i", i=4)
             src = raw[a, r0][:, :, c0 - r0 : c1 - r0].rearrange("p t (c i) -> p c t i", i=4)
@@ -102,7 +103,6 @@ def tile_list_tab4_none_kernel(tc, tab, w, offs, out):
             nc.sync.dma_start(out[P * n : P * n + P, :], result[:])
 
         on_scalar, on_vector = nc.scalar.copy, nc.vector.tensor_copy
-        H = M // 2
 
         load_words(0)
         load_weights(0, 0, H)
@@ -121,36 +121,45 @@ def tile_list_tab4_none_kernel(tc, tab, w, offs, out):
         quantise(0, 0, 0, M)
         multiply(0, 0, M)
 
+        load_weights(3, 0, H)
         load_words(2)
-        load_weights(3, 0, M)
+        load_weights(4, 0, H)
+        load_weights(5, 0, H)
         pick_scales(1)
         pick_scales(2)
         shift_scales(1, 3)
-        for c0 in (0, H):
-            load_weights(4, c0, c0 + H)
-            load_weights(5, c0, c0 + H)
+        load_weights(3, H, M)
+        load_weights(4, H, M)
+        load_weights(5, H, H + P)
+        load_weights(5, H + P, M)
 
         pick_words(1)
-        for a in (1, 2):
-            interleave(on_scalar, a, 0, 0, 0, M)
-            quantise(a, 0, 0, M)
-            multiply(a, 0, M)
-        pick_words(2)
+        interleave(on_scalar, 1, 0, 0, 0, M)
+        quantise(1, 0, 0, M)
+        multiply(1, 0, M)
+        interleave(on_scalar, 2, 0, 0, 0, 448)
+        interleave(on_vector, 2, 0, 0, 448, M)
+        quantise(2, 0, 0, M)
+        multiply(2, 0, M)
 
-        interleave(on_scalar, 3, 0, 0, 0, H)
-        interleave(on_scalar, 3, 0, 0, H, 448)
-        interleave(on_vector, 3, 0, 0, 448, M)
-        for c0 in (0, H):
-            quantise(3, 0, c0, c0 + H)
-            multiply(3, c0, c0 + H)
-
-        for c0 in (0, H):
-            for a in (4, 5):
-                split = c0 + (160 if c0 and a == 5 else 192)
-                interleave(on_scalar, a, c0, c0, c0, split)
-                interleave(on_vector, a, c0, c0, split, c0 + H)
-                quantise(a, c0, c0, c0 + H)
-                multiply(a, c0, c0 + H)
-        for n in range(3):
-            store(on_scalar, n)
-        store(on_vector, 3)
+        for a in (3, 4, 5):
+            interleave(on_scalar, a, 0, 0, 0, H)
+            quantise(a, 0, 0, H)
+            multiply(a, 0, H)
+            if a == 3:
+                pick_words(2)
+        for a, split in ((3, H + 176), (4, H + 144)):
+            interleave(on_scalar, a, H, H, H, split)
+            interleave(on_vector, a, H, H, split, M)
+            quantise(a, H, H, M)
+            multiply(a, H, M)
+        interleave(on_scalar, 5, H, H, H, H + P)
+        quantise(5, H, H, H + P)
+        multiply(5, H, H + P)
+        store(on_scalar, 0)
+        interleave(on_vector, 5, H + P, H + P, H + P, M)
+        quantise(5, H + P, H + P, M)
+        multiply(5, H + P, M)
+        store(on_scalar, 1)
+        store(on_vector, 2)
+        store(on_scalar, 3)

@@ -39,7 +39,7 @@ def tile_list_tab4_none_kernel(tc, tab, w, offs, out):
         nc.scalar.copy(warm[:, 1:2], warm[:, 0:1])
 
         banks = [psum.tile([P, S], F32, name=f"bank{n}") for n in range(4)]
-        words, parted, raw, grouped, codes, scales = {}, {}, {}, {}, {}, {}
+        words, picked, parted, raw, grouped, codes, scales = {}, {}, {}, {}, {}, {}, {}
 
         def load_words(m):
             words[m] = keep.tile([P, T], I32, name=f"words{m}", align_bytes=64)
@@ -57,10 +57,12 @@ def tile_list_tab4_none_kernel(tc, tab, w, offs, out):
             nc.sync.dma_start(raw[key][:], rows.rearrange("(p j) c -> p j c", j=4))
 
         def pick_words(m):
-            picked = keep.tile([P, S], I32, name=f"picked{m}", align_bytes=64)
-            nc.vector.tensor_copy(picked[:].bitcast(U32), words[m][:].bitcast(U32).indirect(offsets[:]))
+            picked[m] = keep.tile([P, S], I32, name=f"picked{m}", align_bytes=64)
+            nc.vector.tensor_copy(picked[m][:].bitcast(U32), words[m][:].bitcast(U32).indirect(offsets[:]))
+
+        def part_words(m):
             parted[m] = keep.tile([P, 2, 2 * S], U8, name=f"parted{m}", align_bytes=64)
-            nc.vector.tensor_copy(parted[m][:].bitcast(U16), picked[:].bitcast(U16).rearrange("p (j h) -> p h j", h=2))
+            nc.vector.tensor_copy(parted[m][:].bitcast(U16), picked[m][:].bitcast(U16).rearrange("p (j h) -> p h j", h=2))
 
         def pick_scales(m):
             nc.vector.tensor_copy(picked_scales[:, m, :], scale_table[:, m, :].indirect(offsets[:]))
@@ -70,7 +72,7 @@ def tile_list_tab4_none_kernel(tc, tab, w, offs, out):
 
         def interleave(copy, a, r0, g0, c0, c1):
             if (a, g0) not in grouped:
-                width = M if a < 3 else P if a == 5 and g0 else H
+                width = M if a < 4 else P if a == 5 and g0 else H
                 grouped[a, g0] = keep.tile([P, width, 4], BF16, name=f"grouped{a}_{g0}", align_bytes=64)
             dst = grouped[a, g0][:, c0 - g0 : c1 - g0, :].rearrange("p (c i) t -> p c t i", i=4)
             src = raw[a, r0][:, :, c0 - r0 : c1 - r0].rearrange("p t (c i) -> p c t i", i=4)
@@ -105,35 +107,34 @@ def tile_list_tab4_none_kernel(tc, tab, w, offs, out):
         on_scalar, on_vector = nc.scalar.copy, nc.vector.tensor_copy
 
         load_words(0)
-        load_weights(0, 0, H)
-        load_weights(0, H, M)
+        load_weights(0, 0, M)
         for q in range(4):
             load_scales(q)
-        load_words(1)
         load_weights(1, 0, M)
+        load_words(1)
         load_weights(2, 0, M)
 
         pick_words(0)
+        part_words(0)
         pick_scales(0)
         shift_scales(0, 1)
-        interleave(on_scalar, 0, 0, 0, 0, H)
-        interleave(on_scalar, 0, H, 0, H, M)
+        interleave(on_scalar, 0, 0, 0, 0, M)
+        pick_scales(1)
         quantise(0, 0, 0, M)
         multiply(0, 0, M)
 
-        load_weights(3, 0, H)
+        load_weights(3, 0, M)
         load_words(2)
         load_weights(4, 0, H)
-        load_weights(5, 0, H)
-        pick_scales(1)
+        pick_words(1)
         pick_scales(2)
         shift_scales(1, 3)
-        load_weights(3, H, M)
+        part_words(1)
+        load_weights(5, 0, H)
         load_weights(4, H, M)
         load_weights(5, H, H + P)
         load_weights(5, H + P, M)
 
-        pick_words(1)
         interleave(on_scalar, 1, 0, 0, 0, M)
         quantise(1, 0, 0, M)
         multiply(1, 0, M)
@@ -142,24 +143,30 @@ def tile_list_tab4_none_kernel(tc, tab, w, offs, out):
         quantise(2, 0, 0, M)
         multiply(2, 0, M)
 
-        for a in (3, 4, 5):
-            interleave(on_scalar, a, 0, 0, 0, H)
-            quantise(a, 0, 0, H)
-            multiply(a, 0, H)
-            if a == 3:
-                pick_words(2)
-        for a, split in ((3, H + 176), (4, H + 144)):
-            interleave(on_scalar, a, H, H, H, split)
-            interleave(on_vector, a, H, H, split, M)
-            quantise(a, H, H, M)
-            multiply(a, H, M)
+        pick_words(2)
+        interleave(on_scalar, 3, 0, 0, 0, H)
+        quantise(3, 0, 0, H)
+        part_words(2)
+        multiply(3, 0, H)
+        interleave(on_scalar, 3, 0, 0, H, M)
+        quantise(3, 0, H, M)
+        multiply(3, H, M)
+
+        interleave(on_scalar, 4, 0, 0, 0, H)
+        quantise(4, 0, 0, H)
+        multiply(4, 0, H)
+        for a, c0 in ((5, 0), (4, H)):
+            interleave(on_scalar, a, c0, c0, c0, c0 + 144)
+            interleave(on_vector, a, c0, c0, c0 + 144, c0 + H)
+            quantise(a, c0, c0, c0 + H)
+            multiply(a, c0, c0 + H)
         interleave(on_scalar, 5, H, H, H, H + P)
         quantise(5, H, H, H + P)
         multiply(5, H, H + P)
-        store(on_scalar, 0)
-        interleave(on_vector, 5, H + P, H + P, H + P, M)
+        store(on_vector, 1)
+        interleave(on_scalar, 5, H + P, H + P, H + P, M)
         quantise(5, H + P, H + P, M)
         multiply(5, H + P, M)
-        store(on_scalar, 1)
+        store(on_scalar, 0)
         store(on_vector, 2)
         store(on_scalar, 3)

from contextlib import ExitStack

import concourse.mybir as mybir

F32 = mybir.dt.float32
BF16 = mybir.dt.bfloat16
I32 = mybir.dt.int32
U32 = mybir.dt.uint32
U16 = mybir.dt.uint16
U8 = mybir.dt.uint8
FP8X4 = mybir.dt.float8_e4m3fn_x4
FP4X4 = mybir.dt.float4_e2m1fn_x4

K, M, T, S = 3072, 512, 1024, 512
P = 128
K_PASS = 512
PASSES = K // K_PASS
PAIRS = PASSES // 2
H = M // 2
FLOPS = 2 * K * M * S


def tile_list_tab4_none_kernel(tc, tab, w, offs, out):
    nc = tc.nc
    with ExitStack() as ctx:
        keep = ctx.enter_context(tc.tile_pool(name="keep", bufs=1))
        psum = ctx.enter_context(tc.psum_pool(name="psum", bufs=1))

        offsets = keep.tile([P, S // 16], U16, name="offsets")
        nc.sync.dma_start(offsets[:], offs)

        scale_table = keep.tile([P, PAIRS, T], U8, name="scale_table", align_bytes=64)
        nc.gpsimd.memset(scale_table[:].bitcast(I32), 0)
        shifted = keep.tile([P, PAIRS, S], U8, name="shifted", align_bytes=64)
        nc.gpsimd.memset(shifted[:].bitcast(I32), 0)
        picked_scales = keep.tile([P, PAIRS, S], U8, name="picked_scales", align_bytes=64)
        warm = keep.tile([P, 2], F32, name="warm")
        nc.vector.memset(warm[:, 0:1], 0.0)
        nc.scalar.copy(warm[:, 1:2], warm[:, 0:1])

        banks = [psum.tile([P, S], F32, name=f"bank{n}") for n in range(4)]
        words, picked, parted, raw, grouped, codes, scales = {}, {}, {}, {}, {}, {}, {}

        def load_words(m):
            words[m] = keep.tile([P, T], I32, name=f"words{m}", align_bytes=64)
            nc.sync.dma_start(words[m][:], tab[m, 0 : 512 * T].bitcast(I32).rearrange("(p t) -> p t", p=P))

        def load_scales(q):
            first = 512 * T + 4 * q * T
            src = tab[:, first : first + 20 * T].bitcast(I32).rearrange("m (i t) -> i m t", i=20)
            nc.sync.dma_start(scale_table[32 * q : 32 * q + 20, :, :].bitcast(I32), src)

        def load_weights(a, c0, c1):
            key = (a, c0)
            raw[key] = keep.tile([P, 4, c1 - c0], F32, name=f"raw{a}_{c0}", align_bytes=64)
            rows = w[K_PASS * a : K_PASS * (a + 1), c0:c1]
            nc.sync.dma_start(raw[key][:], rows.rearrange("(p j) c -> p j c", j=4))

        def pick_words(m):
            picked[m] = keep.tile([P, S], I32, name=f"picked{m}", align_bytes=64)
            nc.vector.tensor_copy(picked[m][:].bitcast(U32), words[m][:].bitcast(U32).indirect(offsets[:]))

        def part_words(m):
            parted[m] = keep.tile([P, 2, 2 * S], U8, name=f"parted{m}", align_bytes=64)
            nc.vector.tensor_copy(parted[m][:].bitcast(U16), picked[m][:].bitcast(U16).rearrange("p (j h) -> p h j", h=2))

        def pick_scales(m):
            nc.vector.tensor_copy(picked_scales[:, m, :], scale_table[:, m, :].indirect(offsets[:]))

        def shift_scales(m0, m1):
            nc.sync.dma_start(shifted[0:112, m0:m1, :].bitcast(I32), picked_scales[16:128, m0:m1, :].bitcast(I32))

        def interleave(copy, a, r0, g0, c0, c1):
            if (a, g0) not in grouped:
                width = M if a < 4 else P if a == 5 and g0 else H
                grouped[a, g0] = keep.tile([P, width, 4], BF16, name=f"grouped{a}_{g0}", align_bytes=64)
            dst = grouped[a, g0][:, c0 - g0 : c1 - g0, :].rearrange("p (c i) t -> p c t i", i=4)
            src = raw[a, r0][:, :, c0 - r0 : c1 - r0].rearrange("p t (c i) -> p c t i", i=4)
            copy(out=dst, in_=src)

        def quantise(a, g0, c0, c1):
            key = (a, c0)
            codes[key] = keep.tile([P, c1 - c0], U32, name=f"codes{a}_{c0}", align_bytes=64)
            scales[key] = keep.tile([P, c1 - c0], U8, name=f"scales{a}_{c0}", align_bytes=64)
            in_ = grouped[a, g0][:, c0 - g0 : c1 - g0, :].rearrange("p c t -> p (c t)")
            nc.vector.quantize_mx(out=codes[key][:].bitcast(FP8X4), scales=scales[key][:], in_=in_)

        def multiply(a, c0, c1):
            m, h = a // 2, a % 2
            moving_scales = shifted if h else picked_scales
            for c in range(0, c1 - c0, P):
                nc.tensor.matmul_mx(
                    out=banks[(c0 + c) // P][:],
                    lhsT=codes[a, c0][:, c : c + P].bitcast(FP8X4),
                    lhsT_scale=scales[a, c0][:, c : c + P],
                    rhs=parted[m][:, h, :].bitcast(FP4X4),
                    rhs_scale=moving_scales[:, m, :],
                    start=(a == 0),
                    stop=(a == PASSES - 1),
                )

        def store(copy, n):
            result = keep.tile([P, S], F32, name=f"result{n}")
            copy(result[:], banks[n][:])
            nc.sync.dma_start(out[P * n : P * n + P, :], result[:])

        on_scalar, on_vector = nc.scalar.copy, nc.vector.tensor_copy

        load_words(0)
        load_weights(0, 0, M)
        for q in range(4):
            load_scales(q)
        load_weights(1, 0, M)
        load_words(1)
        load_weights(2, 0, M)

        pick_words(0)
        part_words(0)
        pick_scales(0)
        shift_scales(0, 1)
        interleave(on_scalar, 0, 0, 0, 0, M)
        pick_scales(1)
        quantise(0, 0, 0, M)
        multiply(0, 0, M)

        load_weights(3, 0, M)
        load_words(2)
        load_weights(4, 0, H)
        pick_words(1)
        pick_scales(2)
        shift_scales(1, 3)
        part_words(1)
        load_weights(5, 0, H)
        load_weights(4, H, M)
        load_weights(5, H, H + P)
        load_weights(5, H + P, M)

        interleave(on_scalar, 1, 0, 0, 0, M)
        quantise(1, 0, 0, M)
        multiply(1, 0, M)
        interleave(on_scalar, 2, 0, 0, 0, 448)
        interleave(on_vector, 2, 0, 0, 448, M)
        quantise(2, 0, 0, M)
        multiply(2, 0, M)

        pick_words(2)
        interleave(on_scalar, 3, 0, 0, 0, H)
        quantise(3, 0, 0, H)
        part_words(2)
        multiply(3, 0, H)
        interleave(on_scalar, 3, 0, 0, H, M)
        quantise(3, 0, H, M)
        multiply(3, H, M)

        interleave(on_scalar, 4, 0, 0, 0, H)
        quantise(4, 0, 0, H)
        multiply(4, 0, H)
        for a, c0 in ((5, 0), (4, H)):
            interleave(on_scalar, a, c0, c0, c0, c0 + 144)
            interleave(on_vector, a, c0, c0, c0 + 144, c0 + H)
            quantise(a, c0, c0, c0 + H)
            multiply(a, c0, c0 + H)
        interleave(on_scalar, 5, H, H, H, H + P)
        quantise(5, H, H, H + P)
        multiply(5, H, H + P)
        store(on_vector, 1)
        interleave(on_scalar, 5, H + P, H + P, H + P, M)
        quantise(5, H + P, H + P, M)
        multiply(5, H + P, M)
        store(on_scalar, 0)
        store(on_vector, 2)
        store(on_scalar, 3)
